import numpy as np, ml_dtypes
CORES = [9,17,57,81,121,137,145,185,209,249]
N = 10
import mx_ref
NC, KT, G, WT = 256, 1, 2, 1
C = np.float32(0.037)
BF = ml_dtypes.bfloat16
def cut(t, i, w=512):
    return t[:, w * i:w * i + w]
def tile(rs):
    return np.stack(rs, axis=2).reshape(128, -1).astype(BF)
def layer(w, X):
    out = []
    for i in range(G):
        for t in range(len(X)):
            p = mx_ref.matmul(mx_ref.quantize(cut(w, len(X) * i + t)), X[t])
            z = p if t == 0 else z + p
        out.append(z)
    return out
def act(Z):
    return [np.maximum(s * z, 0) * C for z in Z for s in (1, -1)]
def setup_inputs(rng):
    def f(*shape):
        return mx_ref.flush((rng.standard_normal(shape, dtype=np.float32) * np.exp2(rng.integers(-2, 3, shape[:-1] + (1,)))).astype(BF))
    return {"x": f(N, 128, KT * 4 * NC), "w1": f(N, 128, G * KT * 512), "w2": f(N, 128, WT * 512)}
def setup_inputs_blocks(rng):
    d = setup_inputs(rng)
    for k in ("x", "w1", "w2"): d[k] = mx_ref.spread(d[k], rng, 4)
    return d
def setup_inputs_wide(rng):
    d = setup_inputs(rng)
    for k in ("x", "w1", "w2"): d[k] = mx_ref.flush((d[k].astype(np.float32) * np.exp2(rng.integers(-8, 9, (N, 1, 1))).astype(np.float32)).astype(BF))
    return d
def setup_inputs_zeros(rng):
    d = setup_inputs(rng); v = d["x"].reshape(N, 128, -1, 4).copy()
    v[np.broadcast_to((rng.random((N, 1, v.shape[2], 1)) < 0.33), v.shape)] = 0
    d["x"] = v.reshape(d["x"].shape)
    return d
def reference(x, w1, w2):
    H = [mx_ref.quantize(tile(act(layer(w1[j], [mx_ref.quantize(cut(x[j], t, 4 * NC)) for t in range(KT)])))) for j in range(N)]
    y = np.zeros((N, 128, N * WT * NC), np.float32)
    for r in range(N):
        for i in range(WT):
            qw = mx_ref.quantize(cut(w2[r], i))
            for j in range(N):
                y[r][:, NC * (WT * j + i):NC * (WT * j + i) + NC] = mx_ref.matmul(qw, H[j])
    return {"y": y}

@@ -1,0 +1,207 @@
+from concourse.bass import DstId, RemoteDMATransfer
+from concourse.mybir import dt, AluOpType, ActivationFunctionType
+
+N = 10
+NC = 256
+C = 0.037
+BANK = 512
+NBANKS = 8
+
+SCRATCH = {
+    "xs": ("sbuf", [128, 4 * NC], "bfloat16"),
+    "w1s": ("sbuf", [128, 1024], "bfloat16"),
+    "w2s": ("sbuf", [128, 512], "bfloat16"),
+    "xq": ("sbuf", [128, NC], "float8_e4m3fn_x4"),
+    "xp": ("sbuf", [128, NC], "uint8"),
+    "w1q": ("sbuf", [128, 256], "float8_e4m3fn_x4"),
+    "w1p": ("sbuf", [128, 256], "uint8"),
+    "w2q": ("sbuf", [128, 128], "float8_e4m3fn_x4"),
+    "w2p": ("sbuf", [128, 128], "uint8"),
+    "ht": ("sbuf", [128, 4 * NC], "bfloat16"),
+    "hq": ("sbuf", [128, N * NC], "float8_e4m3fn_x4"),
+    "hp": ("sbuf", [128, N * NC], "uint8"),
+    "ps": ("psum", [128, NBANKS * BANK], "float32"),
+    "ys": ("sbuf", [128, N * NC], "float32"),
+}
+SEMAPHORES = (["lx", "lw0", "lw1", "lw2", "qx", "qw0", "qw1", "qw2", "z0", "z1a", "z1b", "act", "hr", "snt", "st"]
+              + ["p%d" % j for j in range(N)] + ["a%d" % j for j in range(N)]
+              + ["m%d" % k for k in range(N)] + ["c%d" % k for k in range(N)])
+
+UNITS = ((0, 3), (1, 2), (1, 2), (0, 2))
+RELAYED = ()
+_CACHE = {}
+
+
+def _subsets(items, size):
+    if size == 0:
+        return [[]]
+    out = []
+    for i in range(len(items) - size + 1):
+        out += [[items[i]] + rest for rest in _subsets(items[i + 1:], size - 1)]
+    return out
+
+
+def _engines(topo, src, dsts):
+    mask = topo.mask(src, dsts[0])
+    for d in dsts[1:]:
+        mask &= topo.mask(src, d)
+    return mask, bin(mask).count("1")
+
+
+def _plan(T, topo):
+    if "plan" in _CACHE:
+        return _CACHE["plan"]
+    cores = [int(c) for c in T.cores]
+    n = len(cores)
+    dists = list(range(1, n))
+    own_count = sum(c for die, c in UNITS if die == 0)
+
+    def load(group):
+        cross = [sum(0 if topo.same_plane(cores[s], cores[(s + k) % n]) else 1 for k in group) for s in range(n)]
+        return max(cross), max(len(group) - c for c in cross)
+
+    best = None
+    for near in _subsets(dists, own_count):
+        far = [k for k in dists if k not in near]
+        a, b = load(near), load(far)
+        key = (max(a[0], b[0]), max(a[1], b[1]))
+        if best is None or key < best[0]:
+            best = (key, near, far)
+    left = {0: list(best[1]), 1: list(best[2])}
+    turns = []
+    when = {}
+    for u, (die, count) in enumerate(UNITS):
+        turns.append(left[die][:count])
+        left[die] = left[die][count:]
+        for t, k in enumerate(turns[u]):
+            when[k] = (u + 1) + 2 * (t + 1) + (4 if (u, t) in RELAYED else 0)
+
+    world = range((max(topo.host(c) for c in cores) + 1) * topo.CORES_PER_HOST)
+    free = {}
+    for d, c in enumerate(cores):
+        for k in world:
+            if topo.mates(k, c) and topo.may_write(k, c):
+                free.setdefault((d, topo.die(k)), []).append(k)
+    pass_on, order = {}, {}
+    for s, c in enumerate(cores):
+        able = [k for k in world if k != c and topo.host(k) == topo.host(c) and topo.chip(k) == topo.chip(c)
+                and all(topo.may_write(k, d) for d in cores)]
+        pool = {0: [k for k in able if topo.die(k) == topo.die(c)], 1: [k for k in able if topo.die(k) != topo.die(c)]}
+        pass_on[c] = (s, [])
+        for u, (die, count) in enumerate(UNITS):
+            h = pool[die].pop(0)
+            pass_on[c][1].append(h)
+            pass_on[h] = (s, [])
+            for t, k in enumerate(turns[u]):
+                d = (s + k) % n
+                if (u, t) in RELAYED:
+                    relay = free[(d, topo.die(h))].pop(0)
+                    pass_on[h][1].append(relay)
+                    pass_on[relay] = (s, [cores[d]])
+                else:
+                    pass_on[h][1].append(cores[d])
+        order[s] = [s] + [(s - k) % n for k in sorted(dists, key=lambda k: (when[k], k))]
+    lands = {}
+    for src in pass_on:
+        j, dsts = pass_on[src]
+        for d in dsts:
+            lands[(j, d)] = _engines(topo, src, dsts)[1]
+    _CACHE["plan"] = (pass_on, lands, order)
+    return _CACHE["plan"]
+
+
+def _send(g, T, topo, core, j, dsts, wait_plane, wait_codes):
+    mask, engines = _engines(topo, core, dsts)
+    ids = []
+    for d in dsts:
+        rid, pid = topo.addr(d, core)
+        ids.append(DstId(rid=rid, pnc=pid))
+    plane = T.hp[:, NC * j:NC * j + NC]
+    codes = T.hq[:, NC * j:NC * j + NC].bitcast(dt.uint8)
+    g.wait_ge(wait_plane[0], wait_plane[1])
+    g.remote_dma_fused([RemoteDMATransfer(dst_ids=ids, dma_engine_mask=mask, remote_sem=T.sem["p%d" % j],
+                                          srcs=[plane], dsts=[plane for d in dsts])], local_sem=T.sem.snt)
+    if wait_codes is not None:
+        g.wait_ge(wait_codes[0], wait_codes[1])
+    g.remote_dma_fused([RemoteDMATransfer(dst_ids=ids, dma_engine_mask=mask, remote_sem=T.sem["a%d" % j],
+                                          srcs=[codes], dsts=[codes for d in dsts])], local_sem=T.sem.snt)
+    g.wait_ge(T.sem.snt, 2 * engines)
+
+
+def rank_program(g, core, T, topo):
+    pass_on, lands, order = _plan(T, topo)
+    S = T.sem
+    r = T.rank_of(core)
+
+    if r is None:
+        if core in pass_on:
+            j, dsts = pass_on[core]
+            got = lands[(j, core)]
+            _send(g, T, topo, core, j, dsts, (S["p%d" % j], got), (S["a%d" % j], got))
+        return
+
+    v, sc, te, sy = g.vector, g.scalar, g.tensor, g.sync
+    relu, copy = ActivationFunctionType.Relu, ActivationFunctionType.Copy
+    own = slice(NC * r, NC * r + NC)
+
+    sy.dma_start(T.xs[:, :], T.x[:, :]).then_inc(S.lx, 16)
+    sc.dma_start(T.w1s[:, 0:512], T.w1[:, 0:512]).then_inc(S.lw0, 16)
+    sy.dma_start(T.w1s[:, 512:1024], T.w1[:, 512:1024]).then_inc(S.lw1, 16)
+    sy.dma_start(T.w2s[:, :], T.w2[:, :]).then_inc(S.lw2, 16)
+
+    v.wait_ge(S.lx, 16)
+    v.quantize_mx(T.xq[:, :], T.xp[:, :], T.xs[:, :]).then_inc(S.qx, 1)
+    v.wait_ge(S.lw0, 16)
+    v.quantize_mx(T.w1q[:, 0:128], T.w1p[:, 0:128], T.w1s[:, 0:512]).then_inc(S.qw0, 1)
+    v.wait_ge(S.lw1, 16)
+    v.quantize_mx(T.w1q[:, 128:256], T.w1p[:, 128:256], T.w1s[:, 512:1024]).then_inc(S.qw1, 1)
+
+    half = NC // 2
+    te.wait_ge(S.qx, 1)
+    te.wait_ge(S.qw0, 1)
+    te.matmul_mx(T.ps[:, 0:NC], T.w1q[:, 0:128], T.w1p[:, 0:128], T.xq[:, :], T.xp[:, :], True, True).then_inc(S.z0, 1)
+    te.wait_ge(S.qw1, 1)
+    te.matmul_mx(T.ps[:, BANK:BANK + half], T.w1q[:, 128:256], T.w1p[:, 128:256],
+                 T.xq[:, 0:half], T.xp[:, 0:half], True, True).then_inc(S.z1a, 1)
+    te.matmul_mx(T.ps[:, 2 * BANK:2 * BANK + half], T.w1q[:, 128:256], T.w1p[:, 128:256],
+                 T.xq[:, half:NC], T.xp[:, half:NC], True, True).then_inc(S.z1b, 1)
+
+    sc.wait_ge(S.z0, 1)
+    sc.activation(T.ht[:, 0:4 * NC:4], T.ps[:, 0:NC], relu, scale=C).then_inc(S.act, 1)
+    sc.activation(T.ht[:, 1:4 * NC:4], T.ps[:, 0:NC], relu, scale=-C).then_inc(S.act, 1)
+    sc.wait_ge(S.z1b, 1)
+    sc.activation(T.ht[:, 4 * half + 2:4 * NC:4], T.ps[:, 2 * BANK:2 * BANK + half], relu, scale=C).then_inc(S.act, 1)
+    sc.activation(T.ht[:, 4 * half + 3:4 * NC:4], T.ps[:, 2 * BANK:2 * BANK + half], relu, scale=-C).then_inc(S.act, 1)
+    v.wait_ge(S.z1a, 1)
+    v.tensor_scalar(T.ht[:, 2:4 * half:4], T.ps[:, BANK:BANK + half], 0.0, C, AluOpType.max, AluOpType.mult).then_inc(S.act, 1)
+    v.tensor_scalar(T.ht[:, 3:4 * half:4], T.ps[:, BANK:BANK + half], -C, 0.0, AluOpType.mult, AluOpType.max).then_inc(S.act, 1)
+    v.wait_ge(S.act, 6)
+    v.quantize_mx(T.hq[:, own], T.hp[:, own], T.ht[:, :]).then_inc(S.hr, 1)
+    v.wait_ge(S.lw2, 16)
+    v.quantize_mx(T.w2q[:, :], T.w2p[:, :], T.w2s[:, :]).then_inc(S.qw2, 1)
+
+    _send(g, T, topo, core, r, pass_on[core][1], (S.hr, 1), None)
+
+    te.wait_ge(S.hr, 1)
+    te.wait_ge(S.act, 6)
+    te.wait_ge(S.qw2, 1)
+    first = 3
+    for k, j in enumerate(order[r]):
+        blk = slice(NC * j, NC * j + NC)
+        bank = (first + k) % NBANKS
+        out = T.ps[:, BANK * bank:BANK * bank + NC]
+        if j != r:
+            te.wait_ge(S["p%d" % j], lands[(j, core)])
+            te.wait_ge(S["a%d" % j], lands[(j, core)])
+        if k >= NBANKS:
+            te.wait_ge(S["c%d" % (k - NBANKS)], 1)
+        te.matmul_mx(out, T.w2q[:, :], T.w2p[:, :], T.hq[:, blk], T.hp[:, blk], True, True).then_inc(S["m%d" % k], 1)
+        if k % 2 == 0:
+            v.wait_ge(S["m%d" % k], 1)
+            v.tensor_copy(T.ys[:, blk], out).then_inc(S["c%d" % k], 1)
+        else:
+            sc.wait_ge(S["m%d" % k], 1)
+            sc.activation(T.ys[:, blk], out, copy).then_inc(S["c%d" % k], 1)
+        sy.wait_ge(S["c%d" % k], 1)
+        sy.dma_start(T.y[:, blk], T.ys[:, blk]).then_inc(S.st, 16)
+    sy.wait_ge(S.st, 16 * len(order[r]))

@@ -23,12 +23,16 @@ SCRATCH = {
     "ps": ("psum", [128, NBANKS * BANK], "float32"),
     "ys": ("sbuf", [128, N * NC], "float32"),
 }
-SEMAPHORES = (["lx", "lw0", "lw1", "lw2", "qx", "qw0", "qw1", "qw2", "z0", "z1a", "z1b", "act", "hr", "snt", "st"]
-              + ["p%d" % j for j in range(N)] + ["a%d" % j for j in range(N)]
+SEMAPHORES = (["lxa", "lxb", "lw0", "lw1", "lw2", "qxa", "qxb", "qw0", "qw1", "qw2", "z0a", "z1a", "z0b", "z1b", "acta", "actb",
+               "hra", "hrb", "snt", "st"]
+              + ["pa%d" % j for j in range(N)]
+              + ["pb%d" % j for j in range(N)]
+              + ["a%d" % j for j in range(N)]
               + ["m%d" % k for k in range(N)] + ["c%d" % k for k in range(N)])
 
-UNITS = ((0, 3), (1, 2), (1, 2), (0, 2))
-RELAYED = ()
+UNITS = ((0, 2, False), (1, 2, False), (1, 2, False), (0, 2, False), (0, 1, True))
+OFF = 4
+GROUPS = (1, 2, 2, 1, 2, 1)
 _CACHE = {}
 
 
@@ -39,6 +43,12 @@ def _subsets(items, size):
     for i in range(len(items) - size + 1):
         out += [[items[i]] + rest for rest in _subsets(items[i + 1:], size - 1)]
     return out
+
+
+def _perms(items):
+    if not items:
+        return [[]]
+    return [[x] + rest for i, x in enumerate(items) for rest in _perms(items[:i] + items[i + 1:])]
 
 
 def _engines(topo, src, dsts):
@@ -54,7 +64,9 @@ def _plan(T, topo):
     cores = [int(c) for c in T.cores]
     n = len(cores)
     dists = list(range(1, n))
-    own_count = sum(c for die, c in UNITS if die == 0)
+    own_count = sum(c for die, c, p in UNITS if die == 0)
+    plain = [k for k in dists if all(topo.same_plane(cores[s], cores[(s + k) % n]) for s in range(n))][0]
+    seq = sorted(((u + 1) + OFF * (t + 1), t, u) for u, (die, count, p) in enumerate(UNITS) for t in range(count))
 
     def load(group):
         cross = [sum(0 if topo.same_plane(cores[s], cores[(s + k) % n]) else 1 for k in group) for s in range(n)]
@@ -62,45 +74,40 @@ def _plan(T, topo):
 
     best = None
     for near in _subsets(dists, own_count):
+        if plain not in near:
+            continue
         far = [k for k in dists if k not in near]
         a, b = load(near), load(far)
         key = (max(a[0], b[0]), max(a[1], b[1]))
-        if best is None or key < best[0]:
-            best = (key, near, far)
-    left = {0: list(best[1]), 1: list(best[2])}
-    turns = []
-    when = {}
-    for u, (die, count) in enumerate(UNITS):
-        turns.append(left[die][:count])
-        left[die] = left[die][count:]
-        for t, k in enumerate(turns[u]):
-            when[k] = (u + 1) + 2 * (t + 1) + (4 if (u, t) in RELAYED else 0)
+        for pn in _perms([k for k in near if k != plain]):
+            for pf in _perms(far):
+                left = {0: list(pn), 1: list(pf)}
+                ks = [plain if UNITS[u][2] else left[UNITS[u][0]].pop(0) for w, t, u in seq]
+                i, miss = 0, 0
+                for size in GROUPS:
+                    if size == 2 and abs(ks[i] - ks[i + 1]) != 1:
+                        miss += 1
+                    i += size
+                if best is None or (key, miss) < best[0]:
+                    best = ((key, miss), ks)
+    ks = best[1]
+    turns = [[] for u in UNITS]
+    for (w, t, u), k in zip(seq, ks):
+        turns[u].append(k)
 
     world = range((max(topo.host(c) for c in cores) + 1) * topo.CORES_PER_HOST)
-    free = {}
-    for d, c in enumerate(cores):
-        for k in world:
-            if topo.mates(k, c) and topo.may_write(k, c):
-                free.setdefault((d, topo.die(k)), []).append(k)
     pass_on, order = {}, {}
     for s, c in enumerate(cores):
-        able = [k for k in world if k != c and topo.host(k) == topo.host(c) and topo.chip(k) == topo.chip(c)
-                and all(topo.may_write(k, d) for d in cores)]
-        pool = {0: [k for k in able if topo.die(k) == topo.die(c)], 1: [k for k in able if topo.die(k) != topo.die(c)]}
+        chip = [k for k in world if k != c and topo.host(k) == topo.host(c) and topo.chip(k) == topo.chip(c)]
+        able = [k for k in chip if all(topo.may_write(k, d) for d in cores)]
         pass_on[c] = (s, [])
-        for u, (die, count) in enumerate(UNITS):
-            h = pool[die].pop(0)
-            pass_on[c][1].append(h)
-            pass_on[h] = (s, [])
-            for t, k in enumerate(turns[u]):
-                d = (s + k) % n
-                if (u, t) in RELAYED:
-                    relay = free[(d, topo.die(h))].pop(0)
-                    pass_on[h][1].append(relay)
-                    pass_on[relay] = (s, [cores[d]])
-                else:
-                    pass_on[h][1].append(cores[d])
-        order[s] = [s] + [(s - k) % n for k in sorted(dists, key=lambda k: (when[k], k))]
+        for u, (die, count, p) in enumerate(UNITS):
+            dsts = [cores[(s + k) % n] for k in turns[u]]
+            pool = [k for k in chip if k not in pass_on and (k not in able if p else k in able)
+                    and (topo.die(k) == topo.die(c)) == (die == 0) and all(topo.may_write(k, d) for d in dsts)]
+            pass_on[c][1].append(pool[0])
+            pass_on[pool[0]] = (s, dsts)
+        order[s] = [s] + [(s - k) % n for k in ks]
     lands = {}
     for src in pass_on:
         j, dsts = pass_on[src]
@@ -110,22 +117,19 @@ def _plan(T, topo):
     return _CACHE["plan"]
 
 
-def _send(g, T, topo, core, j, dsts, wait_plane, wait_codes):
-    mask, engines = _engines(topo, core, dsts)
+def _write(g, T, topo, core, dsts, mask, sem, view):
     ids = []
     for d in dsts:
         rid, pid = topo.addr(d, core)
         ids.append(DstId(rid=rid, pnc=pid))
-    plane = T.hp[:, NC * j:NC * j + NC]
-    codes = T.hq[:, NC * j:NC * j + NC].bitcast(dt.uint8)
-    g.wait_ge(wait_plane[0], wait_plane[1])
-    g.remote_dma_fused([RemoteDMATransfer(dst_ids=ids, dma_engine_mask=mask, remote_sem=T.sem["p%d" % j],
-                                          srcs=[plane], dsts=[plane for d in dsts])], local_sem=T.sem.snt)
-    if wait_codes is not None:
-        g.wait_ge(wait_codes[0], wait_codes[1])
-    g.remote_dma_fused([RemoteDMATransfer(dst_ids=ids, dma_engine_mask=mask, remote_sem=T.sem["a%d" % j],
-                                          srcs=[codes], dsts=[codes for d in dsts])], local_sem=T.sem.snt)
-    g.wait_ge(T.sem.snt, 2 * engines)
+    g.remote_dma_fused([RemoteDMATransfer(dst_ids=ids, dma_engine_mask=mask, remote_sem=sem,
+                                          srcs=[view], dsts=[view for d in dsts])], local_sem=T.sem.snt)
+
+
+def _views(T, j):
+    half = NC // 2
+    return (T.hp[:, NC * j:NC * j + half], T.hp[:, NC * j + half:NC * j + NC], T.hp[:, NC * j:NC * j + NC],
+            T.hq[:, NC * j:NC * j + NC].bitcast(dt.uint8))
 
 
 def rank_program(g, core, T, topo):
@@ -137,61 +141,117 @@ def rank_program(g, core, T, topo):
         if core in pass_on:
             j, dsts = pass_on[core]
             got = lands[(j, core)]
-            _send(g, T, topo, core, j, dsts, (S["p%d" % j], got), (S["a%d" % j], got))
+            mask, engines = _engines(topo, core, dsts)
+            left, right, plane, codes = _views(T, j)
+            g.wait_ge(S["pa%d" % j], got)
+            _write(g, T, topo, core, dsts[:1], mask, S["pa%d" % j], left)
+            g.wait_ge(S["pb%d" % j], got)
+            _write(g, T, topo, core, dsts[:1], mask, S["pb%d" % j], right)
+            calls = 3
+            if core == pass_on[int(T.cores[j])][1][0]:
+                g.wait_ge(S["a%d" % j], got)
+                _write(g, T, topo, core, dsts[:1], mask, S["a%d" % j], codes)
+                _write(g, T, topo, core, dsts[1:], mask, S["pb%d" % j], plane)
+                _write(g, T, topo, core, dsts[1:], mask, S["a%d" % j], codes)
+                calls = 5
+            else:
+                if dsts[1:]:
+                    _write(g, T, topo, core, dsts[1:], mask, S["pb%d" % j], plane)
+                    calls = 4
+                g.wait_ge(S["a%d" % j], got)
+                _write(g, T, topo, core, dsts, mask, S["a%d" % j], codes)
+            g.wait_ge(S.snt, calls * engines)
         return
 
     v, sc, te, sy = g.vector, g.scalar, g.tensor, g.sync
     relu, copy = ActivationFunctionType.Relu, ActivationFunctionType.Copy
-    own = slice(NC * r, NC * r + NC)
+    half = NC // 2
+    H2 = 4 * half
 
-    sy.dma_start(T.xs[:, :], T.x[:, :]).then_inc(S.lx, 16)
+    sy.dma_start(T.xs[:, 0:H2], T.x[:, 0:H2]).then_inc(S.lxa, 16)
     sc.dma_start(T.w1s[:, 0:512], T.w1[:, 0:512]).then_inc(S.lw0, 16)
     sy.dma_start(T.w1s[:, 512:1024], T.w1[:, 512:1024]).then_inc(S.lw1, 16)
+    sy.dma_start(T.xs[:, H2:2 * H2], T.x[:, H2:2 * H2]).then_inc(S.lxb, 16)
     sy.dma_start(T.w2s[:, :], T.w2[:, :]).then_inc(S.lw2, 16)
 
-    v.wait_ge(S.lx, 16)
-    v.quantize_mx(T.xq[:, :], T.xp[:, :], T.xs[:, :]).then_inc(S.qx, 1)
+    v.wait_ge(S.lxa, 16)
+    v.quantize_mx(T.xq[:, 0:half], T.xp[:, 0:half], T.xs[:, 0:H2]).then_inc(S.qxa, 1)
     v.wait_ge(S.lw0, 16)
     v.quantize_mx(T.w1q[:, 0:128], T.w1p[:, 0:128], T.w1s[:, 0:512]).then_inc(S.qw0, 1)
     v.wait_ge(S.lw1, 16)
     v.quantize_mx(T.w1q[:, 128:256], T.w1p[:, 128:256], T.w1s[:, 512:1024]).then_inc(S.qw1, 1)
 
-    half = NC // 2
-    te.wait_ge(S.qx, 1)
-    te.wait_ge(S.qw0, 1)
-    te.matmul_mx(T.ps[:, 0:NC], T.w1q[:, 0:128], T.w1p[:, 0:128], T.xq[:, :], T.xp[:, :], True, True).then_inc(S.z0, 1)
-    te.wait_ge(S.qw1, 1)
-    te.matmul_mx(T.ps[:, BANK:BANK + half], T.w1q[:, 128:256], T.w1p[:, 128:256],
-                 T.xq[:, 0:half], T.xp[:, 0:half], True, True).then_inc(S.z1a, 1)
-    te.matmul_mx(T.ps[:, 2 * BANK:2 * BANK + half], T.w1q[:, 128:256], T.w1p[:, 128:256],
-                 T.xq[:, half:NC], T.xp[:, half:NC], True, True).then_inc(S.z1b, 1)
+    def z(bank, i, lo, sem):
+        te.matmul_mx(T.ps[:, BANK * bank:BANK * bank + half], T.w1q[:, 128 * i:128 * i + 128], T.w1p[:, 128 * i:128 * i + 128],
+                     T.xq[:, lo:lo + half], T.xp[:, lo:lo + half], True, True).then_inc(sem, 1)
 
-    sc.wait_ge(S.z0, 1)
-    sc.activation(T.ht[:, 0:4 * NC:4], T.ps[:, 0:NC], relu, scale=C).then_inc(S.act, 1)
-    sc.activation(T.ht[:, 1:4 * NC:4], T.ps[:, 0:NC], relu, scale=-C).then_inc(S.act, 1)
-    sc.wait_ge(S.z1b, 1)
-    sc.activation(T.ht[:, 4 * half + 2:4 * NC:4], T.ps[:, 2 * BANK:2 * BANK + half], relu, scale=C).then_inc(S.act, 1)
-    sc.activation(T.ht[:, 4 * half + 3:4 * NC:4], T.ps[:, 2 * BANK:2 * BANK + half], relu, scale=-C).then_inc(S.act, 1)
-    v.wait_ge(S.z1a, 1)
-    v.tensor_scalar(T.ht[:, 2:4 * half:4], T.ps[:, BANK:BANK + half], 0.0, C, AluOpType.max, AluOpType.mult).then_inc(S.act, 1)
-    v.tensor_scalar(T.ht[:, 3:4 * half:4], T.ps[:, BANK:BANK + half], -C, 0.0, AluOpType.mult, AluOpType.max).then_inc(S.act, 1)
-    v.wait_ge(S.act, 6)
-    v.quantize_mx(T.hq[:, own], T.hp[:, own], T.ht[:, :]).then_inc(S.hr, 1)
+    te.wait_ge(S.qxa, 1)
+    te.wait_ge(S.qw0, 1)
+    z(0, 0, 0, S.z0a)
+    te.wait_ge(S.qw1, 1)
+    z(1, 1, 0, S.z1a)
+    te.wait_ge(S.qxb, 1)
+    z(2, 0, half, S.z0b)
+    z(3, 1, half, S.z1b)
+
+    def signs_scalar(bank, b, lo, sem):
+        zz = T.ps[:, BANK * bank:BANK * bank + half]
+        sc.activation(T.ht[:, lo + b:lo + H2:4], zz, relu, scale=C).then_inc(sem, 1)
+        sc.activation(T.ht[:, lo + b + 1:lo + H2:4], zz, relu, scale=-C).then_inc(sem, 1)
+
+    sc.wait_ge(S.z0a, 1)
+    signs_scalar(0, 0, 0, S.acta)
+    sc.wait_ge(S.z1a, 1)
+    signs_scalar(1, 2, 0, S.acta)
+    sc.wait_ge(S.z0b, 1)
+    signs_scalar(2, 0, H2, S.actb)
+
+    lo = NC * r
+    v.wait_ge(S.acta, 4)
+    v.quantize_mx(T.hq[:, lo:lo + half], T.hp[:, lo:lo + half], T.ht[:, 0:H2]).then_inc(S.hra, 1)
+    v.wait_ge(S.lxb, 16)
+    v.quantize_mx(T.xq[:, half:NC], T.xp[:, half:NC], T.xs[:, H2:2 * H2]).then_inc(S.qxb, 1)
+    v.wait_ge(S.z1b, 1)
+    zz = T.ps[:, 3 * BANK:3 * BANK + half]
+    v.tensor_scalar(T.ht[:, H2 + 2:2 * H2:4], zz, 0.0, C, AluOpType.max, AluOpType.mult).then_inc(S.actb, 1)
+    v.tensor_scalar(T.ht[:, H2 + 3:2 * H2:4], zz, -C, 0.0, AluOpType.mult, AluOpType.max).then_inc(S.actb, 1)
+    v.wait_ge(S.actb, 4)
+    v.quantize_mx(T.hq[:, lo + half:lo + NC], T.hp[:, lo + half:lo + NC], T.ht[:, H2:2 * H2]).then_inc(S.hrb, 1)
     v.wait_ge(S.lw2, 16)
     v.quantize_mx(T.w2q[:, :], T.w2p[:, :], T.w2s[:, :]).then_inc(S.qw2, 1)
 
-    _send(g, T, topo, core, r, pass_on[core][1], (S.hr, 1), None)
+    helpers = pass_on[core][1]
+    mask, engines = _engines(topo, core, helpers)
+    left, right, plane, codes = _views(T, r)
+    g.wait_ge(S.hra, 1)
+    _write(g, T, topo, core, helpers, mask, S["pa%d" % r], left)
+    g.wait_ge(S.hrb, 1)
+    _write(g, T, topo, core, helpers[:1], mask, S["pb%d" % r], right)
+    _write(g, T, topo, core, helpers[:1], mask, S["a%d" % r], codes)
+    _write(g, T, topo, core, helpers[1:], mask, S["pb%d" % r], right)
+    _write(g, T, topo, core, helpers[1:], mask, S["a%d" % r], codes)
+    g.wait_ge(S.snt, 5 * engines)
 
-    te.wait_ge(S.hr, 1)
-    te.wait_ge(S.act, 6)
+    te.wait_ge(S.hra, 1)
+    te.wait_ge(S.hrb, 1)
+    te.wait_ge(S.acta, 4)
+    te.wait_ge(S.actb, 4)
     te.wait_ge(S.qw2, 1)
-    first = 3
+    first = 4
+    firsts = [(pass_on[h][0], pass_on[h][1][0]) for h in pass_on if T.rank_of(h) is None]
+    last, at = {0: [0]}, 1
+    for size in GROUPS:
+        last[at + size - 1] = list(range(at, at + size))
+        at += size
+    stores = [0]
     for k, j in enumerate(order[r]):
         blk = slice(NC * j, NC * j + NC)
         bank = (first + k) % NBANKS
         out = T.ps[:, BANK * bank:BANK * bank + NC]
         if j != r:
-            te.wait_ge(S["p%d" % j], lands[(j, core)])
+            if (j, core) in firsts:
+                te.wait_ge(S["pa%d" % j], lands[(j, core)])
+            te.wait_ge(S["pb%d" % j], lands[(j, core)])
             te.wait_ge(S["a%d" % j], lands[(j, core)])
         if k >= NBANKS:
             te.wait_ge(S["c%d" % (k - NBANKS)], 1)
@@ -202,6 +262,13 @@ def rank_program(g, core, T, topo):
         else:
             sc.wait_ge(S["m%d" % k], 1)
             sc.activation(T.ys[:, blk], out, copy).then_inc(S["c%d" % k], 1)
-        sy.wait_ge(S["c%d" % k], 1)
-        sy.dma_start(T.y[:, blk], T.ys[:, blk]).then_inc(S.st, 16)
-    sy.wait_ge(S.st, 16 * len(order[r]))
+        if k in last:
+            for i in last[k]:
+                sy.wait_ge(S["c%d" % i], 1)
+            js = sorted(order[r][i] for i in last[k])
+            runs = [js] if js[-1] - js[0] == len(js) - 1 else [[b] for b in js]
+            for run in runs:
+                cols = slice(NC * run[0], NC * run[-1] + NC)
+                sy.dma_start(T.y[:, cols], T.ys[:, cols]).then_inc(S.st, 16)
+                stores[0] += 1
+    sy.wait_ge(S.st, 16 * stores[0])

from concourse.bass import DstId, RemoteDMATransfer
from concourse.mybir import dt, AluOpType, ActivationFunctionType

N = 10
NC = 256
C = 0.037
BANK = 512
NBANKS = 8

SCRATCH = {
    "xs": ("sbuf", [128, 4 * NC], "bfloat16"),
    "w1s": ("sbuf", [128, 1024], "bfloat16"),
    "w2s": ("sbuf", [128, 512], "bfloat16"),
    "xq": ("sbuf", [128, NC], "float8_e4m3fn_x4"),
    "xp": ("sbuf", [128, NC], "uint8"),
    "w1q": ("sbuf", [128, 256], "float8_e4m3fn_x4"),
    "w1p": ("sbuf", [128, 256], "uint8"),
    "w2q": ("sbuf", [128, 128], "float8_e4m3fn_x4"),
    "w2p": ("sbuf", [128, 128], "uint8"),
    "ht": ("sbuf", [128, 4 * NC], "bfloat16"),
    "hq": ("sbuf", [128, N * NC], "float8_e4m3fn_x4"),
    "hp": ("sbuf", [128, N * NC], "uint8"),
    "ps": ("psum", [128, NBANKS * BANK], "float32"),
    "ys": ("sbuf", [128, N * NC], "float32"),
}
SEMAPHORES = (["lxa", "lxb", "lw0", "lw1", "lw2", "qxa", "qxb", "qw0", "qw1", "qw2", "z0a", "z1a", "z0b", "z1b", "acta", "actb",
               "hra", "hrb", "snt", "st"]
              + ["pa%d" % j for j in range(N)]
              + ["pb%d" % j for j in range(N)]
              + ["a%d" % j for j in range(N)]
              + ["m%d" % k for k in range(N)] + ["c%d" % k for k in range(N)])

UNITS = ((0, 2, False), (1, 2, False), (1, 2, False), (0, 2, False), (0, 1, True))
OFF = 4
GROUPS = (1, 2, 2, 1, 2, 1)
_CACHE = {}


def _subsets(items, size):
    if size == 0:
        return [[]]
    out = []
    for i in range(len(items) - size + 1):
        out += [[items[i]] + rest for rest in _subsets(items[i + 1:], size - 1)]
    return out


def _perms(items):
    if not items:
        return [[]]
    return [[x] + rest for i, x in enumerate(items) for rest in _perms(items[:i] + items[i + 1:])]


def _engines(topo, src, dsts):
    mask = topo.mask(src, dsts[0])
    for d in dsts[1:]:
        mask &= topo.mask(src, d)
    return mask, bin(mask).count("1")


def _plan(T, topo):
    if "plan" in _CACHE:
        return _CACHE["plan"]
    cores = [int(c) for c in T.cores]
    n = len(cores)
    dists = list(range(1, n))
    own_count = sum(c for die, c, p in UNITS if die == 0)
    plain = [k for k in dists if all(topo.same_plane(cores[s], cores[(s + k) % n]) for s in range(n))][0]
    seq = sorted(((u + 1) + OFF * (t + 1), t, u) for u, (die, count, p) in enumerate(UNITS) for t in range(count))

    def load(group):
        cross = [sum(0 if topo.same_plane(cores[s], cores[(s + k) % n]) else 1 for k in group) for s in range(n)]
        return max(cross), max(len(group) - c for c in cross)

    best = None
    for near in _subsets(dists, own_count):
        if plain not in near:
            continue
        far = [k for k in dists if k not in near]
        a, b = load(near), load(far)
        key = (max(a[0], b[0]), max(a[1], b[1]))
        for pn in _perms([k for k in near if k != plain]):
            for pf in _perms(far):
                left = {0: list(pn), 1: list(pf)}
                ks = [plain if UNITS[u][2] else left[UNITS[u][0]].pop(0) for w, t, u in seq]
                i, miss = 0, 0
                for size in GROUPS:
                    if size == 2 and abs(ks[i] - ks[i + 1]) != 1:
                        miss += 1
                    i += size
                if best is None or (key, miss) < best[0]:
                    best = ((key, miss), ks)
    ks = best[1]
    turns = [[] for u in UNITS]
    for (w, t, u), k in zip(seq, ks):
        turns[u].append(k)

    world = range((max(topo.host(c) for c in cores) + 1) * topo.CORES_PER_HOST)
    pass_on, order = {}, {}
    for s, c in enumerate(cores):
        chip = [k for k in world if k != c and topo.host(k) == topo.host(c) and topo.chip(k) == topo.chip(c)]
        able = [k for k in chip if all(topo.may_write(k, d) for d in cores)]
        pass_on[c] = (s, [])
        for u, (die, count, p) in enumerate(UNITS):
            dsts = [cores[(s + k) % n] for k in turns[u]]
            pool = [k for k in chip if k not in pass_on and (k not in able if p else k in able)
                    and (topo.die(k) == topo.die(c)) == (die == 0) and all(topo.may_write(k, d) for d in dsts)]
            pass_on[c][1].append(pool[0])
            pass_on[pool[0]] = (s, dsts)
        order[s] = [s] + [(s - k) % n for k in ks]
    lands = {}
    for src in pass_on:
        j, dsts = pass_on[src]
        for d in dsts:
            lands[(j, d)] = _engines(topo, src, dsts)[1]
    _CACHE["plan"] = (pass_on, lands, order)
    return _CACHE["plan"]


def _write(g, T, topo, core, dsts, mask, sem, view):
    ids = []
    for d in dsts:
        rid, pid = topo.addr(d, core)
        ids.append(DstId(rid=rid, pnc=pid))
    g.remote_dma_fused([RemoteDMATransfer(dst_ids=ids, dma_engine_mask=mask, remote_sem=sem,
                                          srcs=[view], dsts=[view for d in dsts])], local_sem=T.sem.snt)


def _views(T, j):
    half = NC // 2
    return (T.hp[:, NC * j:NC * j + half], T.hp[:, NC * j + half:NC * j + NC], T.hp[:, NC * j:NC * j + NC],
            T.hq[:, NC * j:NC * j + NC].bitcast(dt.uint8))


def rank_program(g, core, T, topo):
    pass_on, lands, order = _plan(T, topo)
    S = T.sem
    r = T.rank_of(core)

    if r is None:
        if core in pass_on:
            j, dsts = pass_on[core]
            got = lands[(j, core)]
            mask, engines = _engines(topo, core, dsts)
            left, right, plane, codes = _views(T, j)
            g.wait_ge(S["pa%d" % j], got)
            _write(g, T, topo, core, dsts[:1], mask, S["pa%d" % j], left)
            g.wait_ge(S["pb%d" % j], got)
            _write(g, T, topo, core, dsts[:1], mask, S["pb%d" % j], right)
            calls = 3
            if core == pass_on[int(T.cores[j])][1][0]:
                g.wait_ge(S["a%d" % j], got)
                _write(g, T, topo, core, dsts[:1], mask, S["a%d" % j], codes)
                _write(g, T, topo, core, dsts[1:], mask, S["pb%d" % j], plane)
                _write(g, T, topo, core, dsts[1:], mask, S["a%d" % j], codes)
                calls = 5
            else:
                if dsts[1:]:
                    _write(g, T, topo, core, dsts[1:], mask, S["pb%d" % j], plane)
                    calls = 4
                g.wait_ge(S["a%d" % j], got)
                _write(g, T, topo, core, dsts, mask, S["a%d" % j], codes)
            g.wait_ge(S.snt, calls * engines)
        return

    v, sc, te, sy = g.vector, g.scalar, g.tensor, g.sync
    relu, copy = ActivationFunctionType.Relu, ActivationFunctionType.Copy
    half = NC // 2
    H2 = 4 * half

    sy.dma_start(T.xs[:, 0:H2], T.x[:, 0:H2]).then_inc(S.lxa, 16)
    sc.dma_start(T.w1s[:, 0:512], T.w1[:, 0:512]).then_inc(S.lw0, 16)
    sy.dma_start(T.w1s[:, 512:1024], T.w1[:, 512:1024]).then_inc(S.lw1, 16)
    sy.dma_start(T.xs[:, H2:2 * H2], T.x[:, H2:2 * H2]).then_inc(S.lxb, 16)
    sy.dma_start(T.w2s[:, :], T.w2[:, :]).then_inc(S.lw2, 16)

    v.wait_ge(S.lxa, 16)
    v.quantize_mx(T.xq[:, 0:half], T.xp[:, 0:half], T.xs[:, 0:H2]).then_inc(S.qxa, 1)
    v.wait_ge(S.lw0, 16)
    v.quantize_mx(T.w1q[:, 0:128], T.w1p[:, 0:128], T.w1s[:, 0:512]).then_inc(S.qw0, 1)
    v.wait_ge(S.lw1, 16)
    v.quantize_mx(T.w1q[:, 128:256], T.w1p[:, 128:256], T.w1s[:, 512:1024]).then_inc(S.qw1, 1)

    def z(bank, i, lo, sem):
        te.matmul_mx(T.ps[:, BANK * bank:BANK * bank + half], T.w1q[:, 128 * i:128 * i + 128], T.w1p[:, 128 * i:128 * i + 128],
                     T.xq[:, lo:lo + half], T.xp[:, lo:lo + half], True, True).then_inc(sem, 1)

    te.wait_ge(S.qxa, 1)
    te.wait_ge(S.qw0, 1)
    z(0, 0, 0, S.z0a)
    te.wait_ge(S.qw1, 1)
    z(1, 1, 0, S.z1a)
    te.wait_ge(S.qxb, 1)
    z(2, 0, half, S.z0b)
    z(3, 1, half, S.z1b)

    def signs_scalar(bank, b, lo, sem):
        zz = T.ps[:, BANK * bank:BANK * bank + half]
        sc.activation(T.ht[:, lo + b:lo + H2:4], zz, relu, scale=C).then_inc(sem, 1)
        sc.activation(T.ht[:, lo + b + 1:lo + H2:4], zz, relu, scale=-C).then_inc(sem, 1)

    sc.wait_ge(S.z0a, 1)
    signs_scalar(0, 0, 0, S.acta)
    sc.wait_ge(S.z1a, 1)
    signs_scalar(1, 2, 0, S.acta)
    sc.wait_ge(S.z0b, 1)
    signs_scalar(2, 0, H2, S.actb)

    lo = NC * r
    v.wait_ge(S.acta, 4)
    v.quantize_mx(T.hq[:, lo:lo + half], T.hp[:, lo:lo + half], T.ht[:, 0:H2]).then_inc(S.hra, 1)
    v.wait_ge(S.lxb, 16)
    v.quantize_mx(T.xq[:, half:NC], T.xp[:, half:NC], T.xs[:, H2:2 * H2]).then_inc(S.qxb, 1)
    v.wait_ge(S.z1b, 1)
    zz = T.ps[:, 3 * BANK:3 * BANK + half]
    v.tensor_scalar(T.ht[:, H2 + 2:2 * H2:4], zz, 0.0, C, AluOpType.max, AluOpType.mult).then_inc(S.actb, 1)
    v.tensor_scalar(T.ht[:, H2 + 3:2 * H2:4], zz, -C, 0.0, AluOpType.mult, AluOpType.max).then_inc(S.actb, 1)
    v.wait_ge(S.actb, 4)
    v.quantize_mx(T.hq[:, lo + half:lo + NC], T.hp[:, lo + half:lo + NC], T.ht[:, H2:2 * H2]).then_inc(S.hrb, 1)
    v.wait_ge(S.lw2, 16)
    v.quantize_mx(T.w2q[:, :], T.w2p[:, :], T.w2s[:, :]).then_inc(S.qw2, 1)

    helpers = pass_on[core][1]
    mask, engines = _engines(topo, core, helpers)
    left, right, plane, codes = _views(T, r)
    g.wait_ge(S.hra, 1)
    _write(g, T, topo, core, helpers, mask, S["pa%d" % r], left)
    g.wait_ge(S.hrb, 1)
    _write(g, T, topo, core, helpers[:1], mask, S["pb%d" % r], right)
    _write(g, T, topo, core, helpers[:1], mask, S["a%d" % r], codes)
    _write(g, T, topo, core, helpers[1:], mask, S["pb%d" % r], right)
    _write(g, T, topo, core, helpers[1:], mask, S["a%d" % r], codes)
    g.wait_ge(S.snt, 5 * engines)

    te.wait_ge(S.hra, 1)
    te.wait_ge(S.hrb, 1)
    te.wait_ge(S.acta, 4)
    te.wait_ge(S.actb, 4)
    te.wait_ge(S.qw2, 1)
    first = 4
    firsts = [(pass_on[h][0], pass_on[h][1][0]) for h in pass_on if T.rank_of(h) is None]
    last, at = {0: [0]}, 1
    for size in GROUPS:
        last[at + size - 1] = list(range(at, at + size))
        at += size
    stores = [0]
    for k, j in enumerate(order[r]):
        blk = slice(NC * j, NC * j + NC)
        bank = (first + k) % NBANKS
        out = T.ps[:, BANK * bank:BANK * bank + NC]
        if j != r:
            if (j, core) in firsts:
                te.wait_ge(S["pa%d" % j], lands[(j, core)])
            te.wait_ge(S["pb%d" % j], lands[(j, core)])
            te.wait_ge(S["a%d" % j], lands[(j, core)])
        if k >= NBANKS:
            te.wait_ge(S["c%d" % (k - NBANKS)], 1)
        te.matmul_mx(out, T.w2q[:, :], T.w2p[:, :], T.hq[:, blk], T.hp[:, blk], True, True).then_inc(S["m%d" % k], 1)
        if k % 2 == 0:
            v.wait_ge(S["m%d" % k], 1)
            v.tensor_copy(T.ys[:, blk], out).then_inc(S["c%d" % k], 1)
        else:
            sc.wait_ge(S["m%d" % k], 1)
            sc.activation(T.ys[:, blk], out, copy).then_inc(S["c%d" % k], 1)
        if k in last:
            for i in last[k]:
                sy.wait_ge(S["c%d" % i], 1)
            js = sorted(order[r][i] for i in last[k])
            runs = [js] if js[-1] - js[0] == len(js) - 1 else [[b] for b in js]
            for run in runs:
                cols = slice(NC * run[0], NC * run[-1] + NC)
                sy.dma_start(T.y[:, cols], T.ys[:, cols]).then_inc(S.st, 16)
                stores[0] += 1
    sy.wait_ge(S.st, 16 * stores[0])
